import numpy as np
import ml_dtypes

BF16 = ml_dtypes.bfloat16


def bf(x):
    return np.asarray(x, np.float32).astype(BF16)


def f32(x):
    return np.asarray(x, np.float32)


def f64(x):
    return np.asarray(x).astype(np.float64)


def striped(idx):
    return np.tile(idx.reshape(-1, 16).T, (8, 1))


S, K, M, N, D, V = 2048, 128, 128, 1024, 4, 256


def setup_inputs():
    return {"table": bf(np.random.standard_normal((K, S))), "w": bf(np.random.standard_normal((K, M)) / np.sqrt(D * K)), "s": f32(0.5 + np.random.random_sample((M, 1))), "b": f32(0.5 * np.random.standard_normal((M, 1))), "offs": striped(np.random.permutation(np.tile(np.arange(S), 2))[:N])}


def reference(table, w, s, b, offs):
    idx = offs[:16].T.reshape(-1)
    x = f64(table)[:, idx]
    y = f64(w).T @ sum(x[:, t * V : (t + 1) * V] for t in range(D))
    return y * f64(s) + f64(b)

import concourse.mybir as mybir

BF16, F32, U16 = mybir.dt.bfloat16, mybir.dt.float32, mybir.dt.uint16
MULT, ADD = mybir.AluOpType.mult, mybir.AluOpType.add

NODES = 2048
FEATURES = 128
OUT_FEATURES = 128
LIST = 1024
NEIGHBOURS = 4
OUT_NODES = LIST // NEIGHBOURS
OFFSETS_PER_COLUMN = 16

FLOPS = 2 * FEATURES * OUT_FEATURES * LIST


def tile_gather_matmul_kernel(tc, table, w, s, b, offs, out):
    nc = tc.nc
    with (
        tc.tile_pool(name="held", bufs=1) as held,
        tc.psum_pool(name="psum", bufs=1) as psum,
    ):
        table_sb = held.tile([FEATURES, NODES], BF16)
        offs_sb = held.tile([FEATURES, LIST // OFFSETS_PER_COLUMN], U16)
        w_sb = held.tile([FEATURES, OUT_FEATURES], BF16)
        s_sb = held.tile([OUT_FEATURES, 1], F32)
        b_sb = held.tile([OUT_FEATURES, 1], F32)

        nc.sync.dma_start(table_sb[:], table)
        nc.sync.dma_start(offs_sb[:], offs)
        nc.scalar.dma_start(w_sb[:], w)
        nc.scalar.dma_start(s_sb[:], s)
        nc.scalar.dma_start(b_sb[:], b)

        y = psum.tile([OUT_FEATURES, OUT_NODES], F32)
        columns = OUT_NODES // OFFSETS_PER_COLUMN
        for t in range(NEIGHBOURS):
            piece = offs_sb[:, t * columns : (t + 1) * columns]
            nc.tensor.matmul(
                y[:],
                w_sb[:],
                table_sb[:].indirect(piece),
                start=(t == 0),
                stop=(t == NEIGHBOURS - 1),
            )

        result = held.tile([OUT_FEATURES, OUT_NODES], F32)
        nc.vector.tensor_scalar(result[:], y[:], s_sb[:], b_sb[:], op0=MULT, op1=ADD)
        nc.sync.dma_start(out, result[:])
